import numpy as np
import ml_dtypes


def mxq(x, axis, fmt="e4m3"):
    dtype, down = {"e4m3": (ml_dtypes.float8_e4m3fn, 7), "e5m2": (ml_dtypes.float8_e5m2, 14)}[fmt]
    v = np.moveaxis(np.asarray(x, np.float32).astype(ml_dtypes.bfloat16).astype(np.float64), axis, -1)
    blocks = v.reshape(v.shape[:-1] + (-1, 32))
    amax = np.abs(blocks).max(-1, keepdims=True)
    byte = np.maximum(np.where(amax > 0, np.frexp(amax)[1] - 1 + 127, 0) - down, 1)
    scale = np.exp2(byte - 127.0)
    codes = (blocks / scale).astype(np.float32).astype(dtype).astype(np.float64)
    return np.moveaxis((codes * scale).reshape(v.shape), -1, axis)


WIDE = False


def mx_kscale(k):
    if not WIDE:
        return np.ones(k)
    levels = np.array([10, -10, 5, -5, 0])
    if k % 512:
        return np.exp2(np.random.permutation(np.resize(levels, k // 32))).repeat(32)
    a = np.empty((k // 512, 16))
    for p in range(k // 512):
        a[p, :8] = np.random.permutation(np.resize(levels, 8))
        for g in range(8):
            far = levels[np.abs(levels - a[p, g]) >= 10]
            a[p, g + 8] = far[np.random.randint(len(far))]
    return np.exp2(a.ravel()).repeat(32)


def f64(x):
    return np.asarray(x).astype(np.float64)


def striped(idx):
    return np.tile(np.asarray(idx).reshape(-1, 16).T, (8, 1)).astype(np.uint16)


def unstriped(offs):
    return offs[:16].T.reshape(-1).astype(np.int64)


def striped8(idx):
    return np.asarray(idx).reshape(8, -1, 16).transpose(0, 2, 1).reshape(128, -1).astype(np.uint16)


def unstriped8(offs):
    return offs.reshape(8, 16, -1).transpose(0, 2, 1).reshape(8, -1).astype(np.int64)


def pick8(x, idx, run):
    r = np.arange(len(x))
    return x[r[:, None], idx[r % (8 * run) // run]]


E2M1 = np.array([0.0, 0.5, 1.0, 1.5, 2.0, 3.0, 4.0, 6.0, -0.0, -0.5, -1.0, -1.5, -2.0, -3.0, -4.0, -6.0])


def pack_weight(w, fmt):
    k, n = w.shape
    w = f64(np.asarray(w, np.float32).astype(ml_dtypes.bfloat16)).reshape(k // 32, 32, n)
    amax = np.abs(w).max(1)
    if fmt == "e4m3":
        byte = np.frexp(amax)[1] - 1 + 127 - 7
    else:
        mant, ex = np.frexp(amax / 6.0)
        byte = np.where(mant > 0.5, ex, ex - 1) + 127
    byte = np.clip(np.where(amax > 0, byte, 1), 1, 254)
    scaled = (w * np.exp2(127.0 - byte)[:, None, :]).reshape(k, n).astype(np.float32)
    by_word = np.ascontiguousarray(scaled.reshape(k // 512, 128, 4, n).transpose(0, 1, 3, 2))
    if fmt == "e4m3":
        words = by_word.astype(ml_dtypes.float8_e4m3fn).view(np.uint8)
    else:
        c = by_word.astype(ml_dtypes.float4_e2m1fn).view(np.uint8) & 0xF
        words = (c[..., 0::2] | (c[..., 1::2] << 4)).reshape(k // 512, 128, 2 * n)
    return np.ascontiguousarray(words), np.ascontiguousarray(byte.astype(np.uint8).reshape(k // 512, 16, n))


def unpack_weight(words, scales, fmt):
    g, _, n = scales.shape
    words = np.ascontiguousarray(words).reshape(g, 128, n, -1)
    if fmt == "e4m3":
        vals = words.view(ml_dtypes.float8_e4m3fn).astype(np.float64)
    else:
        nib = np.empty((g, 128, n, 4), np.uint8)
        nib[..., 0::2] = words & 0xF
        nib[..., 1::2] = words >> 4
        vals = E2M1[nib]
    vals = vals * np.repeat(np.exp2(scales.astype(np.float64) - 127.0), 8, axis=1)[..., None]
    return vals.transpose(0, 1, 3, 2).reshape(g * 512, n)


def sigmoid(v):
    return 1.0 / (1.0 + np.exp(-v))


def sgn(shape):
    return np.random.uniform(0.5, 2.0, shape) * np.where(np.random.standard_normal(shape) < 0, -1.0, 1.0)


K, J, R, T, Z, M, O, C, N, S = 512, 512, 512, 1024, 512, 1024, 192, 256, 256, 1024


def setup_inputs():
    n = np.random.standard_normal
    idx = np.random.permutation(T)[:J]
    idx2 = np.random.permutation(M)[:J]
    idx3 = np.stack([np.random.permutation(J)[:O] for _ in range(8)])
    idx4 = np.stack([np.random.permutation(C)[:O] for _ in range(8)])
    idx5 = np.stack([np.random.permutation(J)[:C] for _ in range(8)])
    idx6 = np.random.permutation(S)[:N]
    fk = mx_kscale(K)
    fr = mx_kscale(R)
    fz = mx_kscale(Z)
    xtp = pack_weight(n((K, T)) * fk[:, None], "e2m1")
    wp = pack_weight(n((K, R)) * 1 / np.sqrt(K) / fk[:, None] * fr, "e4m3")
    xop = pack_weight(n((Z, M)) / fz[:, None], "e4m3")
    w2p = pack_weight(n((Z, R)) * 1 / np.sqrt(Z) * fz[:, None], "e2m1")
    vsp = pack_weight(n((R, S)) * 1 / np.sqrt(R) / fr[:, None], "e2m1")
    return {
        "xt_words": xtp[0],
        "xt_scales": xtp[1],
        "w_words": wp[0],
        "w_scales": wp[1],
        "xo_words": xop[0],
        "xo_scales": xop[1],
        "w2_words": w2p[0],
        "w2_scales": w2p[1],
        "sl": (sgn((R, 1))).astype(np.float32),
        "gf": (np.random.uniform(-1.0, 1.0, (R, 1))).astype(np.float32),
        "sa": (np.random.uniform(0.5, 1.6, (R, 1))).astype(np.float32),
        "vs_words": vsp[0],
        "vs_scales": vsp[1],
        "offs": striped(idx),
        "offs2": striped(idx2),
        "offs3": striped8(idx3),
        "offs4": striped8(idx4),
        "offs5": striped8(idx5),
        "offs6": striped(idx6),
    }


def reference(xt_words, xt_scales, w_words, w_scales, xo_words, xo_scales, w2_words, w2_scales, sl, gf, sa, vs_words, vs_scales, offs, offs2, offs3, offs4, offs5, offs6):
    idx = unstriped(offs)
    idx2 = unstriped(offs2)
    idx3 = unstriped8(offs3)
    idx4 = unstriped8(offs4)
    idx5 = unstriped8(offs5)
    idx6 = unstriped(offs6)
    xtu = unpack_weight(xt_words, xt_scales, "e2m1")
    wu = unpack_weight(w_words, w_scales, "e4m3")
    xou = unpack_weight(xo_words, xo_scales, "e4m3")
    w2u = unpack_weight(w2_words, w2_scales, "e2m1")
    vsu = unpack_weight(vs_words, vs_scales, "e2m1")
    xtidxg = xtu[:, idx]
    a = wu.T @ xtidxg
    xoidx2g = xou[:, idx2]
    b = w2u.T @ xoidx2g
    h1 = pick8(a, idx3, 64) * f64(sa)
    pw = np.zeros((R, C))
    pw[np.arange(R)[:, None], idx4[np.arange(R) % 512 // 64]] = h1
    hid = pw * sigmoid(pick8(b, idx5, 64) * f64(sl) + f64(gf))
    vsidx6g = vsu[:, idx6]
    hidq = mxq(hid, 0, "e4m3")
    y = vsidx6g.T @ hidq
    return y

@@ -1,0 +1,220 @@
+from contextlib import ExitStack
+
+import concourse.mybir as mybir
+
+K, J, R, T, Z, M, O, C, N, S = 512, 512, 512, 1024, 512, 1024, 192, 256, 256, 1024
+FLOPS = 2 * K * R * J + 2 * Z * R * J + 2 * R * N * C
+
+F32 = mybir.dt.float32
+BF16 = mybir.dt.bfloat16
+I32 = mybir.dt.int32
+U32 = mybir.dt.uint32
+U16 = mybir.dt.uint16
+U8 = mybir.dt.uint8
+FP8X4 = mybir.dt.float8_e4m3fn_x4
+FP4X4 = mybir.dt.float4_e2m1fn_x4
+ACT = mybir.ActivationFunctionType
+MULT = mybir.AluOpType.mult
+
+P = 128
+PACK = 4
+HJ = J // 2
+HC = C // 2
+
+
+def tile_picked_tokens_gate_two_gatedfill_store_plain_kernel(
+    tc, xt_words, xt_scales, w_words, w_scales, xo_words, xo_scales, w2_words, w2_scales,
+    sl, gf, sa, vs_words, vs_scales, offs, offs2, offs3, offs4, offs5, offs6, out,
+):
+    nc = tc.nc
+    with ExitStack() as ctx:
+        sb = ctx.enter_context(tc.tile_pool(name="sb", bufs=1))
+        reuse = ctx.enter_context(tc.tile_pool(name="reuse", bufs=1))
+        ps = ctx.enter_context(tc.psum_pool(name="ps", bufs=1))
+
+        def tile(name, width, dtype, tag=""):
+            return sb.tile([P, width], dtype, name=name, tag=tag, align_bytes=64)
+
+        def placed(name, width, dtype, offset):
+            return reuse.tile([P, width], dtype, name=name, offset=offset, align_bytes=64)
+
+        def load_words(t, words):
+            nc.sync.dma_start(out=t[:].bitcast(I32), in_=words.bitcast(I32))
+
+        def load_list(name, src):
+            t = sb.tile([P, src.shape[1]], U16, name=name)
+            nc.sync.dma_start(out=t[:], in_=src)
+            return t
+
+        def load_scales(plane, scales):
+            for q in range(4):
+                nc.sync.dma_start(out=plane[32 * q : 32 * q + 4, :].bitcast(I32), in_=scales[0, 4 * q : 4 * q + 4, :].bitcast(I32))
+
+        def load_rows(name, vec):
+            t = tile(name, PACK, F32)
+            nc.gpsimd.dma_start(out=t[:], in_=vec.rearrange("(p t) o -> p (t o)", t=PACK))
+            return t
+
+        def deal(copy, dst, src, t0, t1):
+            copy(
+                out=dst[:].rearrange("p (t m) -> p m t", t=PACK)[:, :, t0:t1],
+                in_=src[:].rearrange("p (m t) -> p m t", t=PACK)[:, :, t0:t1],
+            )
+
+        warm = tile("warm", 16, F32)
+        nc.gpsimd.memset(warm[:, 0:1], 0.0)
+        nc.scalar.activation(out=warm[:, 8:9], in_=warm[:, 0:1], func=ACT.Sigmoid)
+
+        xts = tile("xts", T, U8)
+        ws = tile("ws", R, U8)
+        xos = placed("xos", M, U8, 4 * M)
+        w2s = tile("w2s", R, U8)
+        vss = tile("vss", S, U8)
+        nc.vector.memset(xts[:].bitcast(I32), 0)
+        nc.gpsimd.memset(ws[:].bitcast(I32), 0)
+        for plane in (xos, w2s, vss):
+            nc.vector.memset(plane[:].bitcast(I32), 0)
+        pw = [tile("pw%d" % t, C, F32) for t in range(PACK)]
+        for t in range(PACK):
+            nc.vector.memset(pw[t][:], 0.0)
+
+        xtw = tile("xtw", T, U16)
+        ww = tile("ww", R, U32)
+        w2w = tile("w2w", R, U16)
+        xow = placed("xow", M, U32, 0)
+        vsw = tile("vsw", S, U16)
+        l1 = load_list("l1", offs)
+        load_words(xtw, xt_words[0])
+        load_scales(xts, xt_scales)
+        load_words(ww, w_words[0].rearrange("p n t -> p (n t)"))
+        load_words(xow, xo_words[0].rearrange("p n t -> p (n t)"))
+        load_scales(ws, w_scales)
+        sa_t = load_rows("sa_t", sa)
+        sl_t = load_rows("sl_t", sl)
+        gf_t = load_rows("gf_t", gf)
+        load_words(w2w, w2_words[0])
+        l2 = load_list("l2", offs2)
+        l3 = load_list("l3", offs3)
+        l4 = load_list("l4", offs4)
+        load_scales(xos, xo_scales)
+        load_scales(w2s, w2_scales)
+        l5 = load_list("l5", offs5)
+        l6 = load_list("l6", offs6)
+        load_words(vsw, vs_words[0])
+        load_scales(vss, vs_scales)
+
+        wwd = tile("wwd", R, U32)
+        deal(nc.scalar.copy, wwd, ww, 0, PACK)
+        w2wd = tile("w2wd", R, U16)
+        deal(nc.scalar.copy, w2wd, w2w, 0, PACK)
+
+        xtg = tile("xtg", J, U16)
+        nc.vector.tensor_copy(out=xtg[:], in_=xtw[:].indirect(l1[:]))
+        xtsg = tile("xtsg", J, U8)
+        wsd = tile("wsd", R, U8)
+        nc.vector.tensor_copy(out=xtsg[:], in_=xts[:].indirect(l1[:]))
+        deal(nc.vector.tensor_copy, wsd, ws, 0, 1)
+        deal(nc.vector.tensor_copy, wsd, ws, 1, PACK)
+
+        a_ps = [ps.tile([P, J], F32, name="a_ps%d" % t, tag="bank%d" % t) for t in range(PACK)]
+        a0_hi = ps.tile([P, HJ], F32, name="a0_hi", tag="bank7")
+        a_sb = [tile("a_sb0", J, F32)] + [placed("a_sb%d" % t, J, F32, 4 * J * (t - 1)) for t in range(1, PACK)]
+
+        def a_product(dst, t, cols):
+            rows = slice(t * P, (t + 1) * P)
+            nc.tensor.matmul_mx(
+                out=dst, lhsT=wwd[:, rows].bitcast(FP8X4), lhsT_scale=wsd[:, rows],
+                rhs=xtg[:, cols].bitcast(FP4X4), rhs_scale=xtsg[:, cols], start=True, stop=True,
+            )
+
+        a_product(a_ps[0][:, :HJ], 0, slice(0, HJ))
+        nc.scalar.copy(out=a_sb[0][:, :HJ], in_=a_ps[0][:, :HJ])
+        a_product(a0_hi[:], 0, slice(HJ, J))
+        nc.scalar.copy(out=a_sb[0][:, HJ:], in_=a0_hi[:])
+        for t in range(1, PACK):
+            a_product(a_ps[t][:], t, slice(0, J))
+
+        b_sb = [tile("b_sb%d" % t, J, F32) for t in range(PACK)]
+        last = PACK - 1
+        h1 = [tile("h1_%d" % t, O, F32) for t in range(last)]
+
+        def fetch(t):
+            nc.scalar.activation(out=h1[t][:], in_=a_sb[t][:].indirect(l3[:]), func=ACT.Copy, scale=sa_t[:, t : t + 1])
+
+        def fill(t):
+            nc.scalar.activation(out=pw[t][:].indirect(l4[:]), in_=h1[t][:], func=ACT.Copy)
+
+        xog = tile("xog", J, U32)
+        xosg = tile("xosg", J, U8)
+        w2sd = tile("w2sd", R, U8)
+        nc.vector.tensor_copy(out=xog[:], in_=xow[:].indirect(l2[:]))
+        nc.vector.tensor_copy(out=a_sb[1][:], in_=a_ps[1][:])
+        nc.vector.tensor_copy(out=a_sb[2][:], in_=a_ps[2][:])
+        nc.vector.tensor_copy(out=xosg[:], in_=xos[:].indirect(l2[:]))
+        deal(nc.vector.tensor_copy, w2sd, w2s, 0, PACK)
+        nc.vector.tensor_copy(out=a_sb[3][:], in_=a_ps[3][:])
+
+        fetch(0)
+        fill(0)
+        fetch(1)
+        fetch(2)
+        fill(1)
+        fill(2)
+
+        for t in range(PACK):
+            rows = slice(t * P, (t + 1) * P)
+            b_ps = ps.tile([P, J], F32, name="b_ps%d" % t, tag="bank%d" % (PACK + t))
+            nc.tensor.matmul_mx(
+                out=b_ps[:], lhsT=w2wd[:, rows].bitcast(FP4X4), lhsT_scale=w2sd[:, rows],
+                rhs=xog[:].bitcast(FP8X4), rhs_scale=xosg[:], start=True, stop=True,
+            )
+            nc.vector.tensor_copy(out=b_sb[t][:], in_=b_ps[:])
+
+        vsg = tile("vsg", N, U16, tag="xog")
+        vssg = tile("vssg", N, U8, tag="xosg")
+        nc.vector.tensor_copy(out=vsg[:], in_=vsw[:].indirect(l6[:]))
+        nc.vector.tensor_copy(out=vssg[:], in_=vss[:].indirect(l6[:]))
+
+        gate = [tile("gate%d" % t, C, F32) for t in range(PACK)]
+
+        def open_gate(t, c0, c1):
+            nc.scalar.activation(
+                out=gate[t][:, c0:c1], in_=b_sb[t][:].indirect(l5[:, c0 // 16 : c1 // 16]), func=ACT.Sigmoid,
+                scale=sl_t[:, t : t + 1], bias=gf_t[:, t : t + 1],
+            )
+
+        planes = sb.tile([P, last, C], BF16, name="planes", align_bytes=64)
+        hid = [sb.tile([P, HC, PACK], BF16, name="hid%d" % h, align_bytes=64) for h in range(2)]
+        for t in range(last):
+            open_gate(t, 0, C)
+            nc.vector.tensor_tensor(out=planes[:, t, :], in0=pw[t][:], in1=gate[t][:], op=MULT)
+        for h in range(2):
+            nc.vector.tensor_copy(out=hid[h][:, :, :last], in_=planes[:, :, h * HC : (h + 1) * HC].rearrange("p t c -> p c t"))
+        h1.append(tile("h1_3", O, F32, tag="b_sb2"))
+        fetch(last)
+        open_gate(last, 0, HC)
+        fill(last)
+        open_gate(last, HC, C)
+
+        hq = [tile("hq%d" % h, HC, U32) for h in range(2)]
+        hs = [tile("hs%d" % h, HC, U8) for h in range(2)]
+        for h in range(2):
+            cols = slice(h * HC, (h + 1) * HC)
+            nc.vector.tensor_tensor(out=hid[h][:, :, last], in0=pw[last][:, cols], in1=gate[last][:, cols], op=MULT)
+        for h in range(2):
+            nc.vector.quantize_mx(out=hq[h][:].bitcast(FP8X4), scales=hs[h][:], in_=hid[h][:].rearrange("p c t -> p (c t)"))
+        for h in range(2):
+            cols = slice(h * HC, (h + 1) * HC)
+            y_sb = sb.tile([P, N // P, HC], F32, name="y_sb%d" % h, align_bytes=64)
+            for m in range(N // P):
+                rows = slice(m * P, (m + 1) * P)
+                y_ps = ps.tile([P, HC], F32, name="y_ps%d%d" % (h, m), tag="bank%d" % (2 * h + m))
+                nc.tensor.matmul_mx(
+                    out=y_ps[:], lhsT=vsg[:, rows].bitcast(FP4X4), lhsT_scale=vssg[:, rows],
+                    rhs=hq[h][:].bitcast(FP8X4), rhs_scale=hs[h][:], start=True, stop=True,
+                )
+                if h == 1 and m == 1:
+                    nc.vector.tensor_copy(out=y_sb[:, m, :], in_=y_ps[:])
+                else:
+                    nc.scalar.copy(out=y_sb[:, m, :], in_=y_ps[:])
+            nc.sync.dma_start(out=out.rearrange("(m p) c -> p m c", p=P)[:, :, cols], in_=y_sb[:])

@@ -38,8 +38,8 @@ def tile_picked_tokens_gate_two_gatedfill_store_plain_kernel(
         def placed(name, width, dtype, offset):
             return reuse.tile([P, width], dtype, name=name, offset=offset, align_bytes=64)
 
-        def load_words(t, words):
-            nc.sync.dma_start(out=t[:].bitcast(I32), in_=words.bitcast(I32))
+        def load_words(queue, t, words):
+            queue.dma_start(out=t[:].bitcast(I32), in_=words.bitcast(I32))
 
         def load_list(name, src):
             t = sb.tile([P, src.shape[1]], U16, name=name)
@@ -84,15 +84,15 @@ def tile_picked_tokens_gate_two_gatedfill_store_plain_kernel(
         xow = placed("xow", M, U32, 0)
         vsw = tile("vsw", S, U16)
         l1 = load_list("l1", offs)
-        load_words(xtw, xt_words[0])
+        load_words(nc.sync, xtw, xt_words[0])
         load_scales(xts, xt_scales)
-        load_words(ww, w_words[0].rearrange("p n t -> p (n t)"))
-        load_words(xow, xo_words[0].rearrange("p n t -> p (n t)"))
+        load_words(nc.sync, ww, w_words[0].rearrange("p n t -> p (n t)"))
+        load_words(nc.sync, xow, xo_words[0].rearrange("p n t -> p (n t)"))
         load_scales(ws, w_scales)
         sa_t = load_rows("sa_t", sa)
+        load_words(nc.gpsimd, w2w, w2_words[0])
         sl_t = load_rows("sl_t", sl)
         gf_t = load_rows("gf_t", gf)
-        load_words(w2w, w2_words[0])
         l2 = load_list("l2", offs2)
         l3 = load_list("l3", offs3)
         l4 = load_list("l4", offs4)
@@ -100,12 +100,12 @@ def tile_picked_tokens_gate_two_gatedfill_store_plain_kernel(
         load_scales(w2s, w2_scales)
         l5 = load_list("l5", offs5)
         l6 = load_list("l6", offs6)
-        load_words(vsw, vs_words[0])
+        load_words(nc.sync, vsw, vs_words[0])
         load_scales(vss, vs_scales)
 
         wwd = tile("wwd", R, U32)
         deal(nc.scalar.copy, wwd, ww, 0, PACK)
-        w2wd = tile("w2wd", R, U16)
+        w2wd = tile("w2wd", R, U16, tag="ww")
         deal(nc.scalar.copy, w2wd, w2w, 0, PACK)
 
         xtg = tile("xtg", J, U16)

from contextlib import ExitStack

import concourse.mybir as mybir

K, J, R, T, Z, M, O, C, N, S = 512, 512, 512, 1024, 512, 1024, 192, 256, 256, 1024
FLOPS = 2 * K * R * J + 2 * Z * R * J + 2 * R * N * C

F32 = mybir.dt.float32
BF16 = mybir.dt.bfloat16
I32 = mybir.dt.int32
U32 = mybir.dt.uint32
U16 = mybir.dt.uint16
U8 = mybir.dt.uint8
FP8X4 = mybir.dt.float8_e4m3fn_x4
FP4X4 = mybir.dt.float4_e2m1fn_x4
ACT = mybir.ActivationFunctionType
MULT = mybir.AluOpType.mult

P = 128
PACK = 4
HJ = J // 2
HC = C // 2


def tile_picked_tokens_gate_two_gatedfill_store_plain_kernel(
    tc, xt_words, xt_scales, w_words, w_scales, xo_words, xo_scales, w2_words, w2_scales,
    sl, gf, sa, vs_words, vs_scales, offs, offs2, offs3, offs4, offs5, offs6, out,
):
    nc = tc.nc
    with ExitStack() as ctx:
        sb = ctx.enter_context(tc.tile_pool(name="sb", bufs=1))
        reuse = ctx.enter_context(tc.tile_pool(name="reuse", bufs=1))
        ps = ctx.enter_context(tc.psum_pool(name="ps", bufs=1))

        def tile(name, width, dtype, tag=""):
            return sb.tile([P, width], dtype, name=name, tag=tag, align_bytes=64)

        def placed(name, width, dtype, offset):
            return reuse.tile([P, width], dtype, name=name, offset=offset, align_bytes=64)

        def load_words(queue, t, words):
            queue.dma_start(out=t[:].bitcast(I32), in_=words.bitcast(I32))

        def load_list(name, src):
            t = sb.tile([P, src.shape[1]], U16, name=name)
            nc.sync.dma_start(out=t[:], in_=src)
            return t

        def load_scales(plane, scales):
            for q in range(4):
                nc.sync.dma_start(out=plane[32 * q : 32 * q + 4, :].bitcast(I32), in_=scales[0, 4 * q : 4 * q + 4, :].bitcast(I32))

        def load_rows(name, vec):
            t = tile(name, PACK, F32)
            nc.gpsimd.dma_start(out=t[:], in_=vec.rearrange("(p t) o -> p (t o)", t=PACK))
            return t

        def deal(copy, dst, src, t0, t1):
            copy(
                out=dst[:].rearrange("p (t m) -> p m t", t=PACK)[:, :, t0:t1],
                in_=src[:].rearrange("p (m t) -> p m t", t=PACK)[:, :, t0:t1],
            )

        warm = tile("warm", 16, F32)
        nc.gpsimd.memset(warm[:, 0:1], 0.0)
        nc.scalar.activation(out=warm[:, 8:9], in_=warm[:, 0:1], func=ACT.Sigmoid)

        xts = tile("xts", T, U8)
        ws = tile("ws", R, U8)
        xos = placed("xos", M, U8, 4 * M)
        w2s = tile("w2s", R, U8)
        vss = tile("vss", S, U8)
        nc.vector.memset(xts[:].bitcast(I32), 0)
        nc.gpsimd.memset(ws[:].bitcast(I32), 0)
        for plane in (xos, w2s, vss):
            nc.vector.memset(plane[:].bitcast(I32), 0)
        pw = [tile("pw%d" % t, C, F32) for t in range(PACK)]
        for t in range(PACK):
            nc.vector.memset(pw[t][:], 0.0)

        xtw = tile("xtw", T, U16)
        ww = tile("ww", R, U32)
        w2w = tile("w2w", R, U16)
        xow = placed("xow", M, U32, 0)
        vsw = tile("vsw", S, U16)
        l1 = load_list("l1", offs)
        load_words(nc.sync, xtw, xt_words[0])
        load_scales(xts, xt_scales)
        load_words(nc.sync, ww, w_words[0].rearrange("p n t -> p (n t)"))
        load_words(nc.sync, xow, xo_words[0].rearrange("p n t -> p (n t)"))
        load_scales(ws, w_scales)
        sa_t = load_rows("sa_t", sa)
        load_words(nc.gpsimd, w2w, w2_words[0])
        sl_t = load_rows("sl_t", sl)
        gf_t = load_rows("gf_t", gf)
        l2 = load_list("l2", offs2)
        l3 = load_list("l3", offs3)
        l4 = load_list("l4", offs4)
        load_scales(xos, xo_scales)
        load_scales(w2s, w2_scales)
        l5 = load_list("l5", offs5)
        l6 = load_list("l6", offs6)
        load_words(nc.sync, vsw, vs_words[0])
        load_scales(vss, vs_scales)

        wwd = tile("wwd", R, U32)
        deal(nc.scalar.copy, wwd, ww, 0, PACK)
        w2wd = tile("w2wd", R, U16, tag="ww")
        deal(nc.scalar.copy, w2wd, w2w, 0, PACK)

        xtg = tile("xtg", J, U16)
        nc.vector.tensor_copy(out=xtg[:], in_=xtw[:].indirect(l1[:]))
        xtsg = tile("xtsg", J, U8)
        wsd = tile("wsd", R, U8)
        nc.vector.tensor_copy(out=xtsg[:], in_=xts[:].indirect(l1[:]))
        deal(nc.vector.tensor_copy, wsd, ws, 0, 1)
        deal(nc.vector.tensor_copy, wsd, ws, 1, PACK)

        a_ps = [ps.tile([P, J], F32, name="a_ps%d" % t, tag="bank%d" % t) for t in range(PACK)]
        a0_hi = ps.tile([P, HJ], F32, name="a0_hi", tag="bank7")
        a_sb = [tile("a_sb0", J, F32)] + [placed("a_sb%d" % t, J, F32, 4 * J * (t - 1)) for t in range(1, PACK)]

        def a_product(dst, t, cols):
            rows = slice(t * P, (t + 1) * P)
            nc.tensor.matmul_mx(
                out=dst, lhsT=wwd[:, rows].bitcast(FP8X4), lhsT_scale=wsd[:, rows],
                rhs=xtg[:, cols].bitcast(FP4X4), rhs_scale=xtsg[:, cols], start=True, stop=True,
            )

        a_product(a_ps[0][:, :HJ], 0, slice(0, HJ))
        nc.scalar.copy(out=a_sb[0][:, :HJ], in_=a_ps[0][:, :HJ])
        a_product(a0_hi[:], 0, slice(HJ, J))
        nc.scalar.copy(out=a_sb[0][:, HJ:], in_=a0_hi[:])
        for t in range(1, PACK):
            a_product(a_ps[t][:], t, slice(0, J))

        b_sb = [tile("b_sb%d" % t, J, F32) for t in range(PACK)]
        last = PACK - 1
        h1 = [tile("h1_%d" % t, O, F32) for t in range(last)]

        def fetch(t):
            nc.scalar.activation(out=h1[t][:], in_=a_sb[t][:].indirect(l3[:]), func=ACT.Copy, scale=sa_t[:, t : t + 1])

        def fill(t):
            nc.scalar.activation(out=pw[t][:].indirect(l4[:]), in_=h1[t][:], func=ACT.Copy)

        xog = tile("xog", J, U32)
        xosg = tile("xosg", J, U8)
        w2sd = tile("w2sd", R, U8)
        nc.vector.tensor_copy(out=xog[:], in_=xow[:].indirect(l2[:]))
        nc.vector.tensor_copy(out=a_sb[1][:], in_=a_ps[1][:])
        nc.vector.tensor_copy(out=a_sb[2][:], in_=a_ps[2][:])
        nc.vector.tensor_copy(out=xosg[:], in_=xos[:].indirect(l2[:]))
        deal(nc.vector.tensor_copy, w2sd, w2s, 0, PACK)
        nc.vector.tensor_copy(out=a_sb[3][:], in_=a_ps[3][:])

        fetch(0)
        fill(0)
        fetch(1)
        fetch(2)
        fill(1)
        fill(2)

        for t in range(PACK):
            rows = slice(t * P, (t + 1) * P)
            b_ps = ps.tile([P, J], F32, name="b_ps%d" % t, tag="bank%d" % (PACK + t))
            nc.tensor.matmul_mx(
                out=b_ps[:], lhsT=w2wd[:, rows].bitcast(FP4X4), lhsT_scale=w2sd[:, rows],
                rhs=xog[:].bitcast(FP8X4), rhs_scale=xosg[:], start=True, stop=True,
            )
            nc.vector.tensor_copy(out=b_sb[t][:], in_=b_ps[:])

        vsg = tile("vsg", N, U16, tag="xog")
        vssg = tile("vssg", N, U8, tag="xosg")
        nc.vector.tensor_copy(out=vsg[:], in_=vsw[:].indirect(l6[:]))
        nc.vector.tensor_copy(out=vssg[:], in_=vss[:].indirect(l6[:]))

        gate = [tile("gate%d" % t, C, F32) for t in range(PACK)]

        def open_gate(t, c0, c1):
            nc.scalar.activation(
                out=gate[t][:, c0:c1], in_=b_sb[t][:].indirect(l5[:, c0 // 16 : c1 // 16]), func=ACT.Sigmoid,
                scale=sl_t[:, t : t + 1], bias=gf_t[:, t : t + 1],
            )

        planes = sb.tile([P, last, C], BF16, name="planes", align_bytes=64)
        hid = [sb.tile([P, HC, PACK], BF16, name="hid%d" % h, align_bytes=64) for h in range(2)]
        for t in range(last):
            open_gate(t, 0, C)
            nc.vector.tensor_tensor(out=planes[:, t, :], in0=pw[t][:], in1=gate[t][:], op=MULT)
        for h in range(2):
            nc.vector.tensor_copy(out=hid[h][:, :, :last], in_=planes[:, :, h * HC : (h + 1) * HC].rearrange("p t c -> p c t"))
        h1.append(tile("h1_3", O, F32, tag="b_sb2"))
        fetch(last)
        open_gate(last, 0, HC)
        fill(last)
        open_gate(last, HC, C)

        hq = [tile("hq%d" % h, HC, U32) for h in range(2)]
        hs = [tile("hs%d" % h, HC, U8) for h in range(2)]
        for h in range(2):
            cols = slice(h * HC, (h + 1) * HC)
            nc.vector.tensor_tensor(out=hid[h][:, :, last], in0=pw[last][:, cols], in1=gate[last][:, cols], op=MULT)
        for h in range(2):
            nc.vector.quantize_mx(out=hq[h][:].bitcast(FP8X4), scales=hs[h][:], in_=hid[h][:].rearrange("p c t -> p (c t)"))
        for h in range(2):
            cols = slice(h * HC, (h + 1) * HC)
            y_sb = sb.tile([P, N // P, HC], F32, name="y_sb%d" % h, align_bytes=64)
            for m in range(N // P):
                rows = slice(m * P, (m + 1) * P)
                y_ps = ps.tile([P, HC], F32, name="y_ps%d%d" % (h, m), tag="bank%d" % (2 * h + m))
                nc.tensor.matmul_mx(
                    out=y_ps[:], lhsT=vsg[:, rows].bitcast(FP4X4), lhsT_scale=vssg[:, rows],
                    rhs=hq[h][:].bitcast(FP8X4), rhs_scale=hs[h][:], start=True, stop=True,
                )
                if h == 1 and m == 1:
                    nc.vector.tensor_copy(out=y_sb[:, m, :], in_=y_ps[:])
                else:
                    nc.scalar.copy(out=y_sb[:, m, :], in_=y_ps[:])
            nc.sync.dma_start(out=out.rearrange("(m p) c -> p m c", p=P)[:, :, cols], in_=y_sb[:])
